import numpy as np, ml_dtypes
CORES = [125,127,253,255,381,383,509,511]
N = 8
GR, GC = 4, 2
L, KA, KB, F = 4, 2, 1, 128
def setup_inputs(rng):
    return {"a": rng.standard_normal((N, 128, KA * 128), dtype=np.float32).astype(ml_dtypes.bfloat16), "b": rng.standard_normal((N, 128, KB * F), dtype=np.float32).astype(ml_dtypes.bfloat16)}
def setup_inputs_big(rng):
    d = setup_inputs(rng)
    for k in ("a", "b"): d[k] = (d[k].astype(np.float32) * 1024.0).astype(d[k].dtype)
    return d
def setup_inputs_small(rng):
    d = setup_inputs(rng)
    for k in ("a", "b"): d[k] = (d[k].astype(np.float32) * (1 / 1024.0)).astype(d[k].dtype)
    return d
def setup_inputs_apart(rng):
    d = setup_inputs(rng)
    f = (10.0 ** rng.permutation(np.linspace(-1.5, 1.5, N))).astype(np.float32).reshape(N, 1, 1)
    for k in ("a", "b"): d[k] = (d[k].astype(np.float32) * f).astype(d[k].dtype)
    return d
def reference(a, b):
    A, B = a.astype(np.float64), b.astype(np.float64)
    y = np.zeros((N, 128, F))
    for i in range(GR):
        for j in range(GC):
            for k in range(L):
                At = A[i * GC + k // KA][:, 128 * (k % KA):128 * (k % KA) + 128]
                Bt = B[(k // KB) * GC + j][:, F * (k % KB):F * (k % KB) + F]
                y[i * GC + j] += At.T @ Bt
    return {"y": y.astype(ml_dtypes.bfloat16 if a.dtype != np.float64 else np.float64)}

from concourse.bass import DstId, RemoteDMATransfer

GR, GC, TW = 4, 2, 128
KA = 2
N_A = 4

SCRATCH = {
    "bd": ("dram", [128, TW], "bfloat16"),
    "ld": ("dram", [128, TW], "bfloat16"),
    "bs": ("sbuf", [128, GR * TW], "bfloat16"),
    "at": ("sbuf", [128, GR * TW], "bfloat16"),
    "ys": ("sbuf", [128, TW], "bfloat16"),
    "ps": ("psum", [128, TW], "float32"),
}
SEMAPHORES = ["bd_ld", "a_ld", "b_ld", "ld_in", "nb_in", "a_in", "opp_in", "ld_cp", "mm", "cp", "st", "left"]


def _bits(mask):
    return [1 << k for k in range(mask.bit_length()) if (mask >> k) & 1]


def _join(bits):
    m = 0
    for b in bits:
        m |= b
    return m


def _ring(T, topo, col):
    ring = [0]
    while len(ring) < GR:
        last = T.cores[ring[-1] * GC + col]
        ring.append([r for r in range(GR) if r not in ring and topo.may_write(last, T.cores[r * GC + col])][0])
    return ring


def rank_program(g, core, T, topo):
    rank = T.rank_of(core)
    if rank is None:
        return
    row, col = rank // GC, rank % GC
    S = T.sem
    ring = _ring(T, topo, col)
    pos, sense = ring.index(row), (1 if col % 2 == 0 else -1)
    nxt, prv, opp = ring[(pos + sense) % GR], ring[(pos - sense) % GR], ring[(pos + 2) % GR]
    c_nxt, c_prv = T.cores[nxt * GC + col], T.cores[prv * GC + col]
    c_par = T.cores[row * GC + (1 - col)]

    def tile(buf, k):
        return buf[:, k * TW:(k + 1) * TW]

    def dst(d):
        rid, pid = topo.addr(d, core)
        return DstId(rid=rid, pnc=pid)

    off = _bits(topo.mask(core, c_nxt) & topo.mask(core, c_prv))
    on_only = _bits(topo.mask(core, c_par) & ~_join(off))
    m_fwd, m_back, m_all, m_a = _join(off[0::2]), _join(off[1::2]), _join(off), _join(on_only[:N_A])
    n_fwd, n_back, n_all = len(off[0::2]), len(off[1::2]), len(off)
    own_a = T.at[:, col * KA * TW:(col + 1) * KA * TW]

    g.sync.dma_start(T.bd[:], T.b[:]).then_inc(S.bd_ld, 16)
    g.sync.dma_start(own_a, T.a[:]).then_inc(S.a_ld, 16)
    g.sync.dma_start(tile(T.bs, row), T.b[:]).then_inc(S.b_ld, 16)

    g.wait_ge(S.bd_ld, 16)
    g.remote_dma_fused([
        RemoteDMATransfer(dst_ids=[dst(c_nxt)], dma_engine_mask=m_fwd, remote_sem=S.ld_in, src=T.bd[:], dst=T.ld[:]),
        RemoteDMATransfer(dst_ids=[dst(c_prv)], dma_engine_mask=m_back, remote_sem=S.nb_in, src=T.bd[:],
                          dst=tile(T.bs, row)),
    ], local_sem=S.left)
    g.wait_ge(S.a_ld, 16)
    rid, pid = topo.addr(c_par, core)
    g.remote_dma(out_ap=own_a, in_ap=own_a, remote_sem=S.a_in, local_sem=S.left, pid=pid, routing_id=rid,
                 dma_engine_mask=m_a)
    g.wait_ge(S.ld_in, n_fwd)
    rid, pid = topo.addr(c_nxt, core)
    g.remote_dma(out_ap=tile(T.bs, prv), in_ap=T.ld[:], remote_sem=S.opp_in, local_sem=S.left, pid=pid, routing_id=rid,
                 dma_engine_mask=m_all)

    g.scalar.wait_ge(S.ld_in, n_fwd)
    g.scalar.dma_start(tile(T.bs, prv), T.ld[:]).then_inc(S.ld_cp, 16)

    b_ready = {row: (S.b_ld, 16), nxt: (S.nb_in, n_back), prv: (S.ld_cp, 16), opp: (S.opp_in, n_all)}
    order = [row, nxt, prv, opp]
    for n, k in enumerate(order):
        g.tensor.wait_ge(*b_ready[k])
        if k // KA == col:
            g.tensor.wait_ge(S.a_ld, 16)
        else:
            g.tensor.wait_ge(S.a_in, N_A)
        mm = g.tensor.matmul(T.ps[:], tile(T.at, k), tile(T.bs, k), start=(n == 0), stop=(n == len(order) - 1))
    mm.then_inc(S.mm, 1)

    g.vector.wait_ge(S.mm, 1)
    g.vector.tensor_copy(T.ys[:], T.ps[:]).then_inc(S.cp, 1)
    g.sync.wait_ge(S.cp, 1)
    g.sync.dma_start(T.y[:], T.ys[:]).then_inc(S.st, 16)
    g.sync.wait_ge(S.st, 16)
    g.wait_ge(S.left, n_fwd + n_back + N_A + n_all)
